import numpy as np
import ml_dtypes


def mxq(x, axis, fmt="e4m3"):
    dtype, down = {"e4m3": (ml_dtypes.float8_e4m3fn, 7), "e5m2": (ml_dtypes.float8_e5m2, 14)}[fmt]
    v = np.moveaxis(np.asarray(x, np.float32).astype(ml_dtypes.bfloat16).astype(np.float64), axis, -1)
    blocks = v.reshape(v.shape[:-1] + (-1, 32))
    amax = np.abs(blocks).max(-1, keepdims=True)
    byte = np.maximum(np.where(amax > 0, np.frexp(amax)[1] - 1 + 127, 0) - down, 1)
    scale = np.exp2(byte - 127.0)
    codes = (blocks / scale).astype(np.float32).astype(dtype).astype(np.float64)
    return np.moveaxis((codes * scale).reshape(v.shape), -1, axis)


WIDE = False


def mx_kscale(k):
    if not WIDE:
        return np.ones(k)
    levels = np.array([10, -10, 5, -5, 0])
    if k % 512:
        return np.exp2(np.random.permutation(np.resize(levels, k // 32))).repeat(32)
    a = np.empty((k // 512, 16))
    for p in range(k // 512):
        a[p, :8] = np.random.permutation(np.resize(levels, 8))
        for g in range(8):
            far = levels[np.abs(levels - a[p, g]) >= 10]
            a[p, g + 8] = far[np.random.randint(len(far))]
    return np.exp2(a.ravel()).repeat(32)


def f64(x):
    return np.asarray(x).astype(np.float64)


def striped(idx):
    return np.tile(idx.reshape(-1, 16).T, (8, 1)).astype(np.uint16)


def unstriped(offs):
    return offs[:16].T.reshape(-1).astype(np.int64)


def silu(v):
    return v / (1.0 + np.exp(-np.maximum(v, -700.0)))


K, T, E, C, N = 2048, 640, 20, 128, 128
TOP = 4


def by_expert(wq, xq):
    return np.concatenate([wq[e].T @ xq[:, e * C:(e + 1) * C] for e in range(E)], axis=1)


def setup_inputs():
    n = np.random.standard_normal
    s = mx_kscale(K)[:, None]
    deal = np.repeat(np.arange(E), C).reshape(TOP, T)[:, np.random.permutation(T)]
    deal = np.take_along_axis(deal, np.argsort(np.random.rand(TOP, T), axis=0), axis=0)
    for _ in range(8):
        s_, t_ = np.random.permutation(T).reshape(2, -1); r = np.random.randint(TOP, size=T // 2); x, y = deal[r, s_].copy(), deal[r, t_].copy()
        ok = ~((deal[:, s_] == y).any(0) | (deal[:, t_] == x).any(0)); deal[r[ok], s_[ok]] = y[ok]; deal[r[ok], t_[ok]] = x[ok]
    order = np.lexsort((np.random.rand(TOP * T), deal.reshape(-1)))
    slot_token = order % T; pos = np.empty(TOP * T, np.int64); pos[order] = np.arange(TOP * T); pos = pos.reshape(TOP, T)
    g = np.random.uniform(0.5, 1.5, (TOP, T)); g = g / g.sum(0)
    w_slot = np.empty(E * C)
    for r in range(TOP): w_slot[pos[r]] = g[r]
    return {
        "xT": (n((K, T)) * s).astype(np.float32),
        "w": (n((E, K, N)) / np.sqrt(K) / s[None]).astype(np.float32),
        "b": (0.3 * n((N, E))).astype(np.float32),
        "gate": np.tile(w_slot, (K, 1)).astype(np.float32),
        "offs": striped(slot_token),
        "pos1": striped(pos[0]),
        "pos2": striped(pos[1]),
        "pos3": striped(pos[2]),
        "pos4": striped(pos[3]),
    }


def reference(xT, w, b, gate, offs, pos1, pos2, pos3, pos4):
    idx = unstriped(offs)
    xq = mxq(f64(gate) * f64(xT)[:, idx], 0, "e4m3")
    y = by_expert(mxq(f64(w), 1, "e4m3"), xq)
    y = silu(y + np.repeat(f64(b), C, axis=1))
    return y[:, unstriped(pos1)] + y[:, unstriped(pos2)] + y[:, unstriped(pos3)] + y[:, unstriped(pos4)]

@@ -1,0 +1,141 @@
+from contextlib import ExitStack
+
+import concourse.mybir as mybir
+
+K, T, E, C, N = 2048, 640, 20, 128, 128
+S = E * C
+FLOPS = 2 * K * N * S
+BYTES = 4 * (K * T + E * K * N + N * E + S + N * T) + 2 * 128 * (S + 4 * T) // 16
+
+F32 = mybir.dt.float32
+BF16 = mybir.dt.bfloat16
+U32 = mybir.dt.uint32
+U16 = mybir.dt.uint16
+U8 = mybir.dt.uint8
+FP8X4 = mybir.dt.float8_e4m3fn_x4
+MULT = mybir.AluOpType.mult
+ADD = mybir.AluOpType.add
+SILU = mybir.ActivationFunctionType.Silu
+
+P = 128
+PACK = 4
+K_PASS = P * PACK
+PASSES = K // K_PASS
+GE = 4
+GS = GE * C
+GROUPS = E // GE
+STEPS = GROUPS * PASSES
+HALF = T // 2
+
+
+def tile_moe_pre_lin_silu_kernel(tc, xT, w, b, gate, offs, pos1, pos2, pos3, pos4, out):
+    nc = tc.nc
+    with ExitStack() as ctx:
+        keep = ctx.enter_context(tc.tile_pool(name="keep", bufs=1))
+        wraw_pool = ctx.enter_context(tc.tile_pool(name="wraw", bufs=5))
+        gath_pool = ctx.enter_context(tc.tile_pool(name="gath", bufs=3))
+        half_pool = ctx.enter_context(tc.tile_pool(name="half", bufs=3))
+        code_pool = ctx.enter_context(tc.tile_pool(name="code", bufs=3))
+        psum = ctx.enter_context(tc.psum_pool(name="psum", bufs=8))
+
+        offs_sb = keep.tile([P, S // 16], U16, name="offs_sb")
+        pos_sb = [keep.tile([P, T // 16], U16, name="pos_sb%d" % r) for r in range(4)]
+        x_sb = [[keep.tile([P, T], F32, name="x_sb%d_%d" % (a, j)) for j in range(PACK)] for a in range(PASSES)]
+        gate_sb = [keep.tile([P, GS], F32, name="gate_sb%d" % g) for g in range(GROUPS)]
+        b_sb = keep.tile([P, E], F32, name="b_sb")
+        y_sb = keep.tile([P, S], F32, name="y_sb")
+
+        x_rows = xT.rearrange("(a p j) t -> a j p t", p=P, j=PACK)
+        w_rows = w.rearrange("(g e) (a p j) n -> g a p e (j n)", e=GE, p=P, j=PACK)
+
+        w_raw = {}
+
+        def load_w(u):
+            w_raw[u] = wraw_pool.tile([P, GE, PACK * N], F32, name="w_raw")
+            nc.sync.dma_start(out=w_raw[u][:], in_=w_rows[u // PASSES, u % PASSES])
+
+        def load_gate(g):
+            nc.sync.dma_start(out=gate_sb[g][:], in_=gate[0:P, g * GS : (g + 1) * GS])
+
+        def load_x(a):
+            for j in range(PACK):
+                nc.sync.dma_start(out=x_sb[a][j][:], in_=x_rows[a, j])
+
+        nc.sync.dma_start(offs_sb[:], offs)
+        load_gate(0)
+        load_x(0)
+        load_x(1)
+        load_w(0)
+        load_x(2)
+        load_w(1)
+        load_x(3)
+        load_w(2)
+        load_gate(1)
+        load_w(3)
+        nc.sync.dma_start(out=b_sb[:], in_=b)
+        for r, pos in enumerate((pos1, pos2, pos3, pos4)):
+            nc.sync.dma_start(pos_sb[r][:], pos)
+        for g in range(2, GROUPS):
+            load_gate(g)
+
+        acc = {}
+        for u in range(STEPS):
+            g, a = divmod(u, PASSES)
+            if u + 4 < STEPS:
+                load_w(u + 4)
+
+            x_slots = gath_pool.tile([P, PACK, GS], F32, name="x_slots")
+            for j in range(PACK):
+                nc.vector.tensor_tensor(
+                    x_slots[:, j, :],
+                    x_sb[a][j][:].indirect(offs_sb[:, g * GS // 16 : (g + 1) * GS // 16]),
+                    gate_sb[g][:],
+                    MULT,
+                )
+
+            w_bf = half_pool.tile([P, GE * N, PACK], BF16, name="w_bf", align_bytes=64)
+            nc.scalar.copy(
+                out=w_bf[:].rearrange("p (e c i) j -> p e c j i", e=GE, i=4),
+                in_=w_raw[u][:].rearrange("p e (j c i) -> p e c j i", j=PACK, i=4),
+            )
+            x_bf = half_pool.tile([P, GS, PACK], BF16, name="x_bf", align_bytes=64)
+            nc.scalar.copy(
+                out=x_bf[:].rearrange("p (c i) j -> p c j i", i=4),
+                in_=x_slots[:].rearrange("p j (c i) -> p c j i", i=4),
+            )
+
+            w_codes = code_pool.tile([P, GE * N], U32, name="w_codes", align_bytes=64)
+            w_scales = code_pool.tile([P, GE * N], U8, name="w_scales", align_bytes=64)
+            nc.vector.quantize_mx(out=w_codes[:].bitcast(FP8X4), scales=w_scales[:], in_=w_bf[:].rearrange("p n j -> p (n j)"))
+            x_codes = code_pool.tile([P, GS], U32, name="x_codes", align_bytes=64)
+            x_scales = code_pool.tile([P, GS], U8, name="x_scales", align_bytes=64)
+            nc.vector.quantize_mx(out=x_codes[:].bitcast(FP8X4), scales=x_scales[:], in_=x_bf[:].rearrange("p s j -> p (s j)"))
+
+            for i in range(GE):
+                e = g * GE + i
+                if a == 0:
+                    acc[e] = psum.tile([P, C], F32, name="acc")
+                nc.tensor.matmul_mx(
+                    out=acc[e][:],
+                    lhsT=w_codes[:, i * N : (i + 1) * N].bitcast(FP8X4),
+                    lhsT_scale=w_scales[:, i * N : (i + 1) * N],
+                    rhs=x_codes[:, i * C : (i + 1) * C].bitcast(FP8X4),
+                    rhs_scale=x_scales[:, i * C : (i + 1) * C],
+                    start=(a == 0),
+                    stop=(a == PASSES - 1),
+                )
+                if a == PASSES - 1:
+                    nc.scalar.activation(y_sb[:, e * C : (e + 1) * C], acc[e][:], SILU, bias=b_sb[:, e : e + 1])
+
+        total = {}
+        for r in range(4):
+            for h in range(2):
+                picked = y_sb[:].indirect(pos_sb[r][:, h * HALF // 16 : (h + 1) * HALF // 16])
+                summed = keep.tile([P, HALF], F32, name="summed%d_%d" % (r, h))
+                if r == 0:
+                    nc.vector.tensor_copy(summed[:], picked)
+                else:
+                    nc.vector.tensor_tensor(summed[:], picked, total[h][:], ADD)
+                total[h] = summed
+        for h in range(2):
+            nc.sync.dma_start(out=out[:, h * HALF : (h + 1) * HALF], in_=total[h][:])

@@ -21,98 +21,120 @@ P = 128
 PACK = 4
 K_PASS = P * PACK
 PASSES = K // K_PASS
-GE = 4
-GS = GE * C
-GROUPS = E // GE
-STEPS = GROUPS * PASSES
+GROUPS = ((0, 8), (8, 8), (16, 4))
+WE = 4
+WINDOW = 8 * C + 16
 HALF = T // 2
+FIRST = 256
 
 
 def tile_moe_pre_lin_silu_kernel(tc, xT, w, b, gate, offs, pos1, pos2, pos3, pos4, out):
     nc = tc.nc
     with ExitStack() as ctx:
         keep = ctx.enter_context(tc.tile_pool(name="keep", bufs=1))
-        wraw_pool = ctx.enter_context(tc.tile_pool(name="wraw", bufs=5))
-        gath_pool = ctx.enter_context(tc.tile_pool(name="gath", bufs=3))
-        half_pool = ctx.enter_context(tc.tile_pool(name="half", bufs=3))
-        code_pool = ctx.enter_context(tc.tile_pool(name="code", bufs=3))
+        wraw_pool = ctx.enter_context(tc.tile_pool(name="wraw", bufs=6))
+        gath_pool = ctx.enter_context(tc.tile_pool(name="gath", bufs=2))
+        half_pool = ctx.enter_context(tc.tile_pool(name="half", bufs=2))
+        code_pool = ctx.enter_context(tc.tile_pool(name="code", bufs=2))
+        sum_pool = ctx.enter_context(tc.tile_pool(name="sums", bufs=4))
         psum = ctx.enter_context(tc.psum_pool(name="psum", bufs=8))
 
         offs_sb = keep.tile([P, S // 16], U16, name="offs_sb")
         pos_sb = [keep.tile([P, T // 16], U16, name="pos_sb%d" % r) for r in range(4)]
-        x_sb = [[keep.tile([P, T], F32, name="x_sb%d_%d" % (a, j)) for j in range(PACK)] for a in range(PASSES)]
-        gate_sb = [keep.tile([P, GS], F32, name="gate_sb%d" % g) for g in range(GROUPS)]
+        x_sb = [[keep.tile([P, WINDOW], F32, name="x_sb%d_%d" % (a, j)) for j in range(PACK)] for a in range(PASSES)]
+        gate_sb = keep.tile([P, S], F32, name="gate_sb")
         b_sb = keep.tile([P, E], F32, name="b_sb")
         y_sb = keep.tile([P, S], F32, name="y_sb")
 
         x_rows = xT.rearrange("(a p j) t -> a j p t", p=P, j=PACK)
-        w_rows = w.rearrange("(g e) (a p j) n -> g a p e (j n)", e=GE, p=P, j=PACK)
+        w_rows = w.rearrange("(q e) (a p j) n -> q a p e (j n)", e=WE, p=P, j=PACK)
 
+        steps = [(e0, ne, a) for e0, ne in GROUPS for a in range(PASSES)]
+        w_loads = [(e0 // WE + q, a) for e0, ne, a in steps for q in range(ne // WE)]
         w_raw = {}
 
-        def load_w(u):
-            w_raw[u] = wraw_pool.tile([P, GE, PACK * N], F32, name="w_raw")
-            nc.sync.dma_start(out=w_raw[u][:], in_=w_rows[u // PASSES, u % PASSES])
+        def load_w(v):
+            if v < len(w_loads):
+                w_raw[w_loads[v]] = wraw_pool.tile([P, WE, PACK * N], F32, name="w_raw")
+                nc.sync.dma_start(out=w_raw[w_loads[v]][:], in_=w_rows[w_loads[v][0], w_loads[v][1]])
 
-        def load_gate(g):
-            nc.sync.dma_start(out=gate_sb[g][:], in_=gate[0:P, g * GS : (g + 1) * GS])
+        def load_gate(s0, s1):
+            nc.sync.dma_start(out=gate_sb[:, s0:s1], in_=gate[0:P, s0:s1])
 
-        def load_x(a):
-            for j in range(PACK):
-                nc.sync.dma_start(out=x_sb[a][j][:], in_=x_rows[a, j])
+        def load_x(a, j):
+            nc.sync.dma_start(out=x_sb[a][j][:, 0:T], in_=x_rows[a, j])
+
 
         nc.sync.dma_start(offs_sb[:], offs)
-        load_gate(0)
-        load_x(0)
-        load_x(1)
-        load_w(0)
-        load_x(2)
-        load_w(1)
-        load_x(3)
-        load_w(2)
-        load_gate(1)
-        load_w(3)
+        load_x(0, 0)
+        load_gate(0, FIRST)
+        load_gate(FIRST, 8 * C)
+        for j in range(1, PACK):
+            load_x(0, j)
+        for a in range(1, PASSES):
+            load_w(2 * a - 2)
+            load_w(2 * a - 1)
+            for j in range(PACK):
+                load_x(a, j)
         nc.sync.dma_start(out=b_sb[:], in_=b)
         for r, pos in enumerate((pos1, pos2, pos3, pos4)):
             nc.sync.dma_start(pos_sb[r][:], pos)
-        for g in range(2, GROUPS):
-            load_gate(g)
+        load_gate(8 * C, S)
+        loaded = 6
 
         acc = {}
-        for u in range(STEPS):
-            g, a = divmod(u, PASSES)
-            if u + 4 < STEPS:
-                load_w(u + 4)
+        pending = []
 
-            x_slots = gath_pool.tile([P, PACK, GS], F32, name="x_slots")
+        def activate():
+            for e in pending:
+                nc.scalar.activation(y_sb[:, e * C : (e + 1) * C], acc[e][:], SILU, bias=b_sb[:, e : e + 1])
+            pending.clear()
+
+        for u, (e0, ne, a) in enumerate(steps):
+            s0, ns = e0 * C, ne * C
+
+            x_slots = gath_pool.tile([P, PACK, ns], F32, name="x_slots")
             for j in range(PACK):
-                nc.vector.tensor_tensor(
-                    x_slots[:, j, :],
-                    x_sb[a][j][:].indirect(offs_sb[:, g * GS // 16 : (g + 1) * GS // 16]),
-                    gate_sb[g][:],
-                    MULT,
+                cuts = (0, FIRST, ns) if u == 0 and j == 0 else (0, ns)
+                for c0, c1 in zip(cuts, cuts[1:]):
+                    nc.vector.tensor_tensor(
+                        x_slots[:, j, c0:c1],
+                        x_sb[a][j][:].indirect(offs_sb[:, (s0 + c0) // 16 : (s0 + c1) // 16]),
+                        gate_sb[:, s0 + c0 : s0 + c1],
+                        MULT,
+                    )
+
+            w_bf = half_pool.tile([P, ne * N, PACK], BF16, name="w_bf", align_bytes=64)
+            for q in range(ne // WE):
+                nc.scalar.copy(
+                    out=w_bf[:, q * WE * N : (q + 1) * WE * N, :].rearrange("p (e c i) j -> p e c j i", e=WE, i=4),
+                    in_=w_raw[e0 // WE + q, a][:].rearrange("p e (j c i) -> p e c j i", j=PACK, i=4),
+                )
+                load_w(loaded)
+                loaded = loaded + 1
+            x_bf = half_pool.tile([P, ns, PACK], BF16, name="x_bf", align_bytes=64)
+            pieces = (0, ns // 2, ns) if u == len(steps) - 1 else (0, ns)
+            for c0, c1 in zip(pieces, pieces[1:]):
+                nc.scalar.copy(
+                    out=x_bf[:, c0:c1, :].rearrange("p (c i) j -> p c j i", i=4),
+                    in_=x_slots[:, :, c0:c1].rearrange("p j (c i) -> p c j i", i=4),
+                )
+            activate()
+
+            w_codes = code_pool.tile([P, ne * N], U32, name="w_codes", align_bytes=64)
+            w_scales = code_pool.tile([P, ne * N], U8, name="w_scales", align_bytes=64)
+            nc.vector.quantize_mx(out=w_codes[:].bitcast(FP8X4), scales=w_scales[:], in_=w_bf[:].rearrange("p n j -> p (n j)"))
+            x_codes = code_pool.tile([P, ns], U32, name="x_codes", align_bytes=64)
+            x_scales = code_pool.tile([P, ns], U8, name="x_scales", align_bytes=64)
+            for c0, c1 in zip(pieces, pieces[1:]):
+                nc.vector.quantize_mx(
+                    out=x_codes[:, c0:c1].bitcast(FP8X4),
+                    scales=x_scales[:, c0:c1],
+                    in_=x_bf[:, c0:c1, :].rearrange("p s j -> p (s j)"),
                 )
 
-            w_bf = half_pool.tile([P, GE * N, PACK], BF16, name="w_bf", align_bytes=64)
-            nc.scalar.copy(
-                out=w_bf[:].rearrange("p (e c i) j -> p e c j i", e=GE, i=4),
-                in_=w_raw[u][:].rearrange("p e (j c i) -> p e c j i", j=PACK, i=4),
-            )
-            x_bf = half_pool.tile([P, GS, PACK], BF16, name="x_bf", align_bytes=64)
-            nc.scalar.copy(
-                out=x_bf[:].rearrange("p (c i) j -> p c j i", i=4),
-                in_=x_slots[:].rearrange("p j (c i) -> p c j i", i=4),
-            )
-
-            w_codes = code_pool.tile([P, GE * N], U32, name="w_codes", align_bytes=64)
-            w_scales = code_pool.tile([P, GE * N], U8, name="w_scales", align_bytes=64)
-            nc.vector.quantize_mx(out=w_codes[:].bitcast(FP8X4), scales=w_scales[:], in_=w_bf[:].rearrange("p n j -> p (n j)"))
-            x_codes = code_pool.tile([P, GS], U32, name="x_codes", align_bytes=64)
-            x_scales = code_pool.tile([P, GS], U8, name="x_scales", align_bytes=64)
-            nc.vector.quantize_mx(out=x_codes[:].bitcast(FP8X4), scales=x_scales[:], in_=x_bf[:].rearrange("p s j -> p (s j)"))
-
-            for i in range(GE):
-                e = g * GE + i
+            for i in range(ne):
+                e = e0 + i
                 if a == 0:
                     acc[e] = psum.tile([P, C], F32, name="acc")
                 nc.tensor.matmul_mx(
@@ -125,13 +147,14 @@ def tile_moe_pre_lin_silu_kernel(tc, xT, w, b, gate, offs, pos1, pos2, pos3, pos
                     stop=(a == PASSES - 1),
                 )
                 if a == PASSES - 1:
-                    nc.scalar.activation(y_sb[:, e * C : (e + 1) * C], acc[e][:], SILU, bias=b_sb[:, e : e + 1])
+                    pending.append(e)
+        activate()
 
         total = {}
         for r in range(4):
             for h in range(2):
                 picked = y_sb[:].indirect(pos_sb[r][:, h * HALF // 16 : (h + 1) * HALF // 16])
-                summed = keep.tile([P, HALF], F32, name="summed%d_%d" % (r, h))
+                summed = sum_pool.tile([P, HALF], F32, name="summed")
                 if r == 0:
                     nc.vector.tensor_copy(summed[:], picked)
                 else:

@@ -4,8 +4,9 @@ import concourse.mybir as mybir
 
 K, T, E, C, N = 2048, 640, 20, 128, 128
 S = E * C
+TOP = 4
 FLOPS = 2 * K * N * S
-BYTES = 4 * (K * T + E * K * N + N * E + S + N * T) + 2 * 128 * (S + 4 * T) // 16
+BYTES = 4 * (K * T + E * K * N + N * E + S + N * T) + 2 * 128 * (S + TOP * T) // 16
 
 F32 = mybir.dt.float32
 BF16 = mybir.dt.bfloat16
@@ -19,44 +20,52 @@ SILU = mybir.ActivationFunctionType.Silu
 
 P = 128
 PACK = 4
-K_PASS = P * PACK
-PASSES = K // K_PASS
-GROUPS = ((0, 8), (8, 8), (16, 4))
-WE = 4
-WINDOW = 8 * C + 16
+PASSES = K // (P * PACK)
+PER_COLUMN = 16
+LINE = 4
+BANKS = 8
+GROUPS = ((0, BANKS), (BANKS, BANKS), (2 * BANKS, E - 2 * BANKS))
+LOAD_EXPERTS = 4
+W_BUFS = 6
+WINDOW = BANKS * C + PER_COLUMN
+FIRST_SLOTS = 320
+LAST_STEP_CUTS = (0, 2 * C, 3 * C, 4 * C)
 HALF = T // 2
-FIRST = 256
+LAST_TOKENS = 96
+
+
+def entries(list_tile, m0, m1):
+    return list_tile[:, m0 // PER_COLUMN : m1 // PER_COLUMN]
 
 
 def tile_moe_pre_lin_silu_kernel(tc, xT, w, b, gate, offs, pos1, pos2, pos3, pos4, out):
     nc = tc.nc
     with ExitStack() as ctx:
         keep = ctx.enter_context(tc.tile_pool(name="keep", bufs=1))
-        wraw_pool = ctx.enter_context(tc.tile_pool(name="wraw", bufs=6))
+        wraw_pool = ctx.enter_context(tc.tile_pool(name="wraw", bufs=W_BUFS))
         gath_pool = ctx.enter_context(tc.tile_pool(name="gath", bufs=2))
         half_pool = ctx.enter_context(tc.tile_pool(name="half", bufs=2))
         code_pool = ctx.enter_context(tc.tile_pool(name="code", bufs=2))
-        sum_pool = ctx.enter_context(tc.tile_pool(name="sums", bufs=4))
-        psum = ctx.enter_context(tc.psum_pool(name="psum", bufs=8))
+        sum_pool = ctx.enter_context(tc.tile_pool(name="sums", bufs=5))
+        psum = ctx.enter_context(tc.psum_pool(name="psum", bufs=BANKS))
 
-        offs_sb = keep.tile([P, S // 16], U16, name="offs_sb")
-        pos_sb = [keep.tile([P, T // 16], U16, name="pos_sb%d" % r) for r in range(4)]
+        offs_sb = keep.tile([P, S // PER_COLUMN], U16, name="offs_sb")
+        pos_sb = [keep.tile([P, T // PER_COLUMN], U16, name="pos_sb%d" % r) for r in range(TOP)]
         x_sb = [[keep.tile([P, WINDOW], F32, name="x_sb%d_%d" % (a, j)) for j in range(PACK)] for a in range(PASSES)]
         gate_sb = keep.tile([P, S], F32, name="gate_sb")
         b_sb = keep.tile([P, E], F32, name="b_sb")
         y_sb = keep.tile([P, S], F32, name="y_sb")
 
         x_rows = xT.rearrange("(a p j) t -> a j p t", p=P, j=PACK)
-        w_rows = w.rearrange("(q e) (a p j) n -> q a p e (j n)", e=WE, p=P, j=PACK)
+        w_rows = w.rearrange("(q e) (a p j) n -> q a p e (j n)", e=LOAD_EXPERTS, p=P, j=PACK)
 
         steps = [(e0, ne, a) for e0, ne in GROUPS for a in range(PASSES)]
-        w_loads = [(e0 // WE + q, a) for e0, ne, a in steps for q in range(ne // WE)]
+        w_loads = [(e0 // LOAD_EXPERTS + q, a) for e0, ne, a in steps for q in range(ne // LOAD_EXPERTS)]
         w_raw = {}
 
         def load_w(v):
-            if v < len(w_loads):
-                w_raw[w_loads[v]] = wraw_pool.tile([P, WE, PACK * N], F32, name="w_raw")
-                nc.sync.dma_start(out=w_raw[w_loads[v]][:], in_=w_rows[w_loads[v][0], w_loads[v][1]])
+            w_raw[w_loads[v]] = wraw_pool.tile([P, LOAD_EXPERTS, PACK * N], F32, name="w_raw")
+            nc.sync.dma_start(out=w_raw[w_loads[v]][:], in_=w_rows[w_loads[v][0], w_loads[v][1]])
 
         def load_gate(s0, s1):
             nc.sync.dma_start(out=gate_sb[:, s0:s1], in_=gate[0:P, s0:s1])
@@ -64,69 +73,71 @@ def tile_moe_pre_lin_silu_kernel(tc, xT, w, b, gate, offs, pos1, pos2, pos3, pos
         def load_x(a, j):
             nc.sync.dma_start(out=x_sb[a][j][:, 0:T], in_=x_rows[a, j])
 
-
         nc.sync.dma_start(offs_sb[:], offs)
         load_x(0, 0)
-        load_gate(0, FIRST)
-        load_gate(FIRST, 8 * C)
+        load_gate(0, FIRST_SLOTS)
+        load_gate(FIRST_SLOTS, BANKS * C)
         for j in range(1, PACK):
             load_x(0, j)
+        loads_a_step = BANKS // LOAD_EXPERTS
         for a in range(1, PASSES):
-            load_w(2 * a - 2)
-            load_w(2 * a - 1)
+            for v in range((a - 1) * loads_a_step, a * loads_a_step):
+                load_w(v)
             for j in range(PACK):
                 load_x(a, j)
         nc.sync.dma_start(out=b_sb[:], in_=b)
         for r, pos in enumerate((pos1, pos2, pos3, pos4)):
             nc.sync.dma_start(pos_sb[r][:], pos)
-        load_gate(8 * C, S)
-        loaded = 6
+        load_gate(BANKS * C, S)
+        next_load = W_BUFS
 
         acc = {}
-        pending = []
+        closed = []
 
-        def activate():
-            for e in pending:
+        def activate_closed():
+            for e in closed:
                 nc.scalar.activation(y_sb[:, e * C : (e + 1) * C], acc[e][:], SILU, bias=b_sb[:, e : e + 1])
-            pending.clear()
+            closed.clear()
 
         for u, (e0, ne, a) in enumerate(steps):
             s0, ns = e0 * C, ne * C
 
             x_slots = gath_pool.tile([P, PACK, ns], F32, name="x_slots")
             for j in range(PACK):
-                cuts = (0, FIRST, ns) if u == 0 and j == 0 else (0, ns)
-                for c0, c1 in zip(cuts, cuts[1:]):
+                gather_cuts = (0, FIRST_SLOTS, ns) if u == 0 and j == 0 else (0, ns)
+                for c0, c1 in zip(gather_cuts, gather_cuts[1:]):
                     nc.vector.tensor_tensor(
                         x_slots[:, j, c0:c1],
-                        x_sb[a][j][:].indirect(offs_sb[:, (s0 + c0) // 16 : (s0 + c1) // 16]),
+                        x_sb[a][j][:].indirect(entries(offs_sb, s0 + c0, s0 + c1)),
                         gate_sb[:, s0 + c0 : s0 + c1],
                         MULT,
                     )
 
             w_bf = half_pool.tile([P, ne * N, PACK], BF16, name="w_bf", align_bytes=64)
-            for q in range(ne // WE):
+            for q in range(ne // LOAD_EXPERTS):
+                columns = slice(q * LOAD_EXPERTS * N, (q + 1) * LOAD_EXPERTS * N)
                 nc.scalar.copy(
-                    out=w_bf[:, q * WE * N : (q + 1) * WE * N, :].rearrange("p (e c i) j -> p e c j i", e=WE, i=4),
-                    in_=w_raw[e0 // WE + q, a][:].rearrange("p e (j c i) -> p e c j i", j=PACK, i=4),
+                    out=w_bf[:, columns, :].rearrange("p (e c i) j -> p e c j i", e=LOAD_EXPERTS, i=LINE),
+                    in_=w_raw[e0 // LOAD_EXPERTS + q, a][:].rearrange("p e (j c i) -> p e c j i", j=PACK, i=LINE),
                 )
-                load_w(loaded)
-                loaded = loaded + 1
+                if next_load < len(w_loads):
+                    load_w(next_load)
+                    next_load = next_load + 1
             x_bf = half_pool.tile([P, ns, PACK], BF16, name="x_bf", align_bytes=64)
-            pieces = (0, ns // 2, ns) if u == len(steps) - 1 else (0, ns)
-            for c0, c1 in zip(pieces, pieces[1:]):
+            step_cuts = LAST_STEP_CUTS if u == len(steps) - 1 else (0, ns)
+            for c0, c1 in zip(step_cuts, step_cuts[1:]):
                 nc.scalar.copy(
-                    out=x_bf[:, c0:c1, :].rearrange("p (c i) j -> p c j i", i=4),
-                    in_=x_slots[:, :, c0:c1].rearrange("p j (c i) -> p c j i", i=4),
+                    out=x_bf[:, c0:c1, :].rearrange("p (c i) j -> p c j i", i=LINE),
+                    in_=x_slots[:, :, c0:c1].rearrange("p j (c i) -> p c j i", i=LINE),
                 )
-            activate()
+            activate_closed()
 
             w_codes = code_pool.tile([P, ne * N], U32, name="w_codes", align_bytes=64)
             w_scales = code_pool.tile([P, ne * N], U8, name="w_scales", align_bytes=64)
             nc.vector.quantize_mx(out=w_codes[:].bitcast(FP8X4), scales=w_scales[:], in_=w_bf[:].rearrange("p n j -> p (n j)"))
             x_codes = code_pool.tile([P, ns], U32, name="x_codes", align_bytes=64)
             x_scales = code_pool.tile([P, ns], U8, name="x_scales", align_bytes=64)
-            for c0, c1 in zip(pieces, pieces[1:]):
+            for c0, c1 in zip(step_cuts, step_cuts[1:]):
                 nc.vector.quantize_mx(
                     out=x_codes[:, c0:c1].bitcast(FP8X4),
                     scales=x_scales[:, c0:c1],
@@ -147,18 +158,22 @@ def tile_moe_pre_lin_silu_kernel(tc, xT, w, b, gate, offs, pos1, pos2, pos3, pos
                     stop=(a == PASSES - 1),
                 )
                 if a == PASSES - 1:
-                    pending.append(e)
-        activate()
+                    closed.append(e)
+        activate_closed()
 
         total = {}
-        for r in range(4):
+        for r in range(TOP - 1):
             for h in range(2):
-                picked = y_sb[:].indirect(pos_sb[r][:, h * HALF // 16 : (h + 1) * HALF // 16])
+                picked = y_sb[:].indirect(entries(pos_sb[r], h * HALF, (h + 1) * HALF))
                 summed = sum_pool.tile([P, HALF], F32, name="summed")
                 if r == 0:
                     nc.vector.tensor_copy(summed[:], picked)
                 else:
                     nc.vector.tensor_tensor(summed[:], picked, total[h][:], ADD)
                 total[h] = summed
-        for h in range(2):
-            nc.sync.dma_start(out=out[:, h * HALF : (h + 1) * HALF], in_=total[h][:])
+        for t0, t1 in ((0, HALF), (HALF, T - LAST_TOKENS), (T - LAST_TOKENS, T)):
+            h = t0 // HALF
+            summed = sum_pool.tile([P, t1 - t0], F32, name="summed")
+            picked = y_sb[:].indirect(entries(pos_sb[TOP - 1], t0, t1))
+            nc.vector.tensor_tensor(summed[:], picked, total[h][:, t0 - h * HALF : t1 - h * HALF], ADD)
+            nc.sync.dma_start(out=out[:, t0:t1], in_=summed[:])

from contextlib import ExitStack

import concourse.mybir as mybir

K, T, E, C, N = 2048, 640, 20, 128, 128
S = E * C
TOP = 4
FLOPS = 2 * K * N * S
BYTES = 4 * (K * T + E * K * N + N * E + S + N * T) + 2 * 128 * (S + TOP * T) // 16

F32 = mybir.dt.float32
BF16 = mybir.dt.bfloat16
U32 = mybir.dt.uint32
U16 = mybir.dt.uint16
U8 = mybir.dt.uint8
FP8X4 = mybir.dt.float8_e4m3fn_x4
MULT = mybir.AluOpType.mult
ADD = mybir.AluOpType.add
SILU = mybir.ActivationFunctionType.Silu

P = 128
PACK = 4
PASSES = K // (P * PACK)
PER_COLUMN = 16
LINE = 4
BANKS = 8
GROUPS = ((0, BANKS), (BANKS, BANKS), (2 * BANKS, E - 2 * BANKS))
LOAD_EXPERTS = 4
W_BUFS = 6
WINDOW = BANKS * C + PER_COLUMN
FIRST_SLOTS = 320
LAST_STEP_CUTS = (0, 2 * C, 3 * C, 4 * C)
HALF = T // 2
LAST_TOKENS = 96


def entries(list_tile, m0, m1):
    return list_tile[:, m0 // PER_COLUMN : m1 // PER_COLUMN]


def tile_moe_pre_lin_silu_kernel(tc, xT, w, b, gate, offs, pos1, pos2, pos3, pos4, out):
    nc = tc.nc
    with ExitStack() as ctx:
        keep = ctx.enter_context(tc.tile_pool(name="keep", bufs=1))
        wraw_pool = ctx.enter_context(tc.tile_pool(name="wraw", bufs=W_BUFS))
        gath_pool = ctx.enter_context(tc.tile_pool(name="gath", bufs=2))
        half_pool = ctx.enter_context(tc.tile_pool(name="half", bufs=2))
        code_pool = ctx.enter_context(tc.tile_pool(name="code", bufs=2))
        sum_pool = ctx.enter_context(tc.tile_pool(name="sums", bufs=5))
        psum = ctx.enter_context(tc.psum_pool(name="psum", bufs=BANKS))

        offs_sb = keep.tile([P, S // PER_COLUMN], U16, name="offs_sb")
        pos_sb = [keep.tile([P, T // PER_COLUMN], U16, name="pos_sb%d" % r) for r in range(TOP)]
        x_sb = [[keep.tile([P, WINDOW], F32, name="x_sb%d_%d" % (a, j)) for j in range(PACK)] for a in range(PASSES)]
        gate_sb = keep.tile([P, S], F32, name="gate_sb")
        b_sb = keep.tile([P, E], F32, name="b_sb")
        y_sb = keep.tile([P, S], F32, name="y_sb")

        x_rows = xT.rearrange("(a p j) t -> a j p t", p=P, j=PACK)
        w_rows = w.rearrange("(q e) (a p j) n -> q a p e (j n)", e=LOAD_EXPERTS, p=P, j=PACK)

        steps = [(e0, ne, a) for e0, ne in GROUPS for a in range(PASSES)]
        w_loads = [(e0 // LOAD_EXPERTS + q, a) for e0, ne, a in steps for q in range(ne // LOAD_EXPERTS)]
        w_raw = {}

        def load_w(v):
            w_raw[w_loads[v]] = wraw_pool.tile([P, LOAD_EXPERTS, PACK * N], F32, name="w_raw")
            nc.sync.dma_start(out=w_raw[w_loads[v]][:], in_=w_rows[w_loads[v][0], w_loads[v][1]])

        def load_gate(s0, s1):
            nc.sync.dma_start(out=gate_sb[:, s0:s1], in_=gate[0:P, s0:s1])

        def load_x(a, j):
            nc.sync.dma_start(out=x_sb[a][j][:, 0:T], in_=x_rows[a, j])

        nc.sync.dma_start(offs_sb[:], offs)
        load_x(0, 0)
        load_gate(0, FIRST_SLOTS)
        load_gate(FIRST_SLOTS, BANKS * C)
        for j in range(1, PACK):
            load_x(0, j)
        loads_a_step = BANKS // LOAD_EXPERTS
        for a in range(1, PASSES):
            for v in range((a - 1) * loads_a_step, a * loads_a_step):
                load_w(v)
            for j in range(PACK):
                load_x(a, j)
        nc.sync.dma_start(out=b_sb[:], in_=b)
        for r, pos in enumerate((pos1, pos2, pos3, pos4)):
            nc.sync.dma_start(pos_sb[r][:], pos)
        load_gate(BANKS * C, S)
        next_load = W_BUFS

        acc = {}
        closed = []

        def activate_closed():
            for e in closed:
                nc.scalar.activation(y_sb[:, e * C : (e + 1) * C], acc[e][:], SILU, bias=b_sb[:, e : e + 1])
            closed.clear()

        for u, (e0, ne, a) in enumerate(steps):
            s0, ns = e0 * C, ne * C

            x_slots = gath_pool.tile([P, PACK, ns], F32, name="x_slots")
            for j in range(PACK):
                gather_cuts = (0, FIRST_SLOTS, ns) if u == 0 and j == 0 else (0, ns)
                for c0, c1 in zip(gather_cuts, gather_cuts[1:]):
                    nc.vector.tensor_tensor(
                        x_slots[:, j, c0:c1],
                        x_sb[a][j][:].indirect(entries(offs_sb, s0 + c0, s0 + c1)),
                        gate_sb[:, s0 + c0 : s0 + c1],
                        MULT,
                    )

            w_bf = half_pool.tile([P, ne * N, PACK], BF16, name="w_bf", align_bytes=64)
            for q in range(ne // LOAD_EXPERTS):
                columns = slice(q * LOAD_EXPERTS * N, (q + 1) * LOAD_EXPERTS * N)
                nc.scalar.copy(
                    out=w_bf[:, columns, :].rearrange("p (e c i) j -> p e c j i", e=LOAD_EXPERTS, i=LINE),
                    in_=w_raw[e0 // LOAD_EXPERTS + q, a][:].rearrange("p e (j c i) -> p e c j i", j=PACK, i=LINE),
                )
                if next_load < len(w_loads):
                    load_w(next_load)
                    next_load = next_load + 1
            x_bf = half_pool.tile([P, ns, PACK], BF16, name="x_bf", align_bytes=64)
            step_cuts = LAST_STEP_CUTS if u == len(steps) - 1 else (0, ns)
            for c0, c1 in zip(step_cuts, step_cuts[1:]):
                nc.scalar.copy(
                    out=x_bf[:, c0:c1, :].rearrange("p (c i) j -> p c j i", i=LINE),
                    in_=x_slots[:, :, c0:c1].rearrange("p j (c i) -> p c j i", i=LINE),
                )
            activate_closed()

            w_codes = code_pool.tile([P, ne * N], U32, name="w_codes", align_bytes=64)
            w_scales = code_pool.tile([P, ne * N], U8, name="w_scales", align_bytes=64)
            nc.vector.quantize_mx(out=w_codes[:].bitcast(FP8X4), scales=w_scales[:], in_=w_bf[:].rearrange("p n j -> p (n j)"))
            x_codes = code_pool.tile([P, ns], U32, name="x_codes", align_bytes=64)
            x_scales = code_pool.tile([P, ns], U8, name="x_scales", align_bytes=64)
            for c0, c1 in zip(step_cuts, step_cuts[1:]):
                nc.vector.quantize_mx(
                    out=x_codes[:, c0:c1].bitcast(FP8X4),
                    scales=x_scales[:, c0:c1],
                    in_=x_bf[:, c0:c1, :].rearrange("p s j -> p (s j)"),
                )

            for i in range(ne):
                e = e0 + i
                if a == 0:
                    acc[e] = psum.tile([P, C], F32, name="acc")
                nc.tensor.matmul_mx(
                    out=acc[e][:],
                    lhsT=w_codes[:, i * N : (i + 1) * N].bitcast(FP8X4),
                    lhsT_scale=w_scales[:, i * N : (i + 1) * N],
                    rhs=x_codes[:, i * C : (i + 1) * C].bitcast(FP8X4),
                    rhs_scale=x_scales[:, i * C : (i + 1) * C],
                    start=(a == 0),
                    stop=(a == PASSES - 1),
                )
                if a == PASSES - 1:
                    closed.append(e)
        activate_closed()

        total = {}
        for r in range(TOP - 1):
            for h in range(2):
                picked = y_sb[:].indirect(entries(pos_sb[r], h * HALF, (h + 1) * HALF))
                summed = sum_pool.tile([P, HALF], F32, name="summed")
                if r == 0:
                    nc.vector.tensor_copy(summed[:], picked)
                else:
                    nc.vector.tensor_tensor(summed[:], picked, total[h][:], ADD)
                total[h] = summed
        for t0, t1 in ((0, HALF), (HALF, T - LAST_TOKENS), (T - LAST_TOKENS, T)):
            h = t0 // HALF
            summed = sum_pool.tile([P, t1 - t0], F32, name="summed")
            picked = y_sb[:].indirect(entries(pos_sb[TOP - 1], t0, t1))
            nc.vector.tensor_tensor(summed[:], picked, total[h][:, t0 - h * HALF : t1 - h * HALF], ADD)
            nc.sync.dma_start(out=out[:, t0:t1], in_=summed[:])
